import numpy as np
import ml_dtypes


def mxq(x, axis, fmt="e4m3"):
    dtype, down = {"e4m3": (ml_dtypes.float8_e4m3fn, 7), "e5m2": (ml_dtypes.float8_e5m2, 14)}[fmt]
    v = np.moveaxis(np.asarray(x, np.float32).astype(ml_dtypes.bfloat16).astype(np.float64), axis, -1)
    blocks = v.reshape(v.shape[:-1] + (-1, 32))
    amax = np.abs(blocks).max(-1, keepdims=True)
    byte = np.maximum(np.where(amax > 0, np.frexp(amax)[1] - 1 + 127, 0) - down, 1)
    scale = np.exp2(byte - 127.0)
    codes = (blocks / scale).astype(np.float32).astype(dtype).astype(np.float64)
    return np.moveaxis((codes * scale).reshape(v.shape), -1, axis)


WIDE = False


def mx_kscale(k):
    if not WIDE:
        return np.ones(k)
    levels = np.array([10, -10, 5, -5, 0])
    if k % 512:
        return np.exp2(np.random.permutation(np.resize(levels, k // 32))).repeat(32)
    a = np.empty((k // 512, 16))
    for p in range(k // 512):
        a[p, :8] = np.random.permutation(np.resize(levels, 8))
        for g in range(8):
            far = levels[np.abs(levels - a[p, g]) >= 10]
            a[p, g + 8] = far[np.random.randint(len(far))]
    return np.exp2(a.ravel()).repeat(32)


def f64(x):
    return np.asarray(x).astype(np.float64)


def striped(idx):
    return np.tile(idx.reshape(-1, 16).T, (8, 1)).astype(np.uint16)


def unstriped(offs):
    return offs[:16].T.reshape(-1).astype(np.int64)


def striped8(idx):
    return np.concatenate([x.reshape(-1, 16).T for x in idx]).astype(np.uint16)


def runs(offs, k):
    lists = np.stack([offs[16 * r : 16 * r + 16].T.reshape(-1) for r in range(8)]).astype(np.int64)
    return lists[np.arange(k) % 512 // 64]


def pack_weight(w):
    k, n = w.shape
    w = f64(np.asarray(w, np.float32).astype(ml_dtypes.bfloat16)).reshape(k // 32, 32, n)
    amax = np.abs(w).max(1)
    byte = np.clip(np.where(amax > 0, np.frexp(amax)[1] - 1 + 127 - 7, 1), 1, 254)
    scaled = (w * np.exp2(127.0 - byte)[:, None, :]).reshape(k, n).astype(np.float32)
    words = np.ascontiguousarray(scaled.reshape(k // 512, 128, 4, n).transpose(0, 1, 3, 2)).astype(ml_dtypes.float8_e4m3fn).view(np.uint8)
    return words, np.ascontiguousarray(byte.astype(np.uint8).reshape(k // 512, 16, n))


def unpack_weight(words, scales):
    g, p, n, _ = words.shape
    vals = np.ascontiguousarray(words).view(ml_dtypes.float8_e4m3fn).astype(np.float64) * np.repeat(np.exp2(scales.astype(np.float64) - 127.0), 8, axis=1)[..., None]
    return vals.transpose(0, 1, 3, 2).reshape(g * 512, n)


def sigmoid(v):
    return 1.0 / (1.0 + np.exp(-np.maximum(v, -700.0)))


K, T, S, N, H, U = 512, 2048, 512, 512, 512, 1024


def setup_inputs():
    n = np.random.standard_normal
    s = mx_kscale(K)[:, None]
    u = mx_kscale(H)
    packed_xT = pack_weight(n((K, T)) * s)
    return {
        "x_words": packed_xT[0],
        "x_scales": packed_xT[1],
        "w1": (n((K, H)) / np.sqrt(K) / s).astype(np.float32),
        "w2": (n((K, H)) / np.sqrt(K) / s).astype(np.float32),
        "gn": (np.random.uniform(0.5, 1.5, (H, 1)) * u[:, None]).astype(np.float32),
        "w3": (n((H, N)) / np.sqrt(H) / u[:, None]).astype(np.float32),
        "mem": n((N, U)).astype(np.float32),
        "offs": striped(np.random.permutation(T)[:S]),
        "hz": striped8(np.random.randint(0, T, (8, S))),
        "n1": striped(np.random.permutation(S)),
        "n2": striped(np.random.permutation(S)),
        "n3": striped8(np.stack([np.random.permutation(U)[:S] for _ in range(8)])),
    }


def reference(x_words, x_scales, w1, w2, gn, w3, mem, offs, hz, n1, n2, n3):
    xq = unpack_weight(x_words, x_scales)[:, unstriped(offs)]
    y = mxq(f64(w1), 0, "e4m3").T @ xq
    x_hz = unpack_weight(x_words, x_scales)[np.arange(K)[:, None], runs(hz, K)]
    d = mxq(f64(w2), 0, "e4m3").T @ x_hz
    z = f64(gn) * ((y + y[:, unstriped(n1)]) * (sigmoid(d + d[:, unstriped(n2)])))
    h = mxq(f64(w3), 0, "e4m3").T @ mxq(z, 0, "e4m3")
    out = f64(mem).copy()
    out[np.arange(N)[:, None], runs(n3, N)] = h
    return out

@@ -1,0 +1,257 @@
+from contextlib import ExitStack
+
+import concourse.mybir as mybir
+from concourse.masks import make_identity
+
+K, T, S, N, H, U = 512, 2048, 512, 512, 512, 1024
+FLOPS = 2 * S * (K * H + K * H + H * N)
+
+F32 = mybir.dt.float32
+BF16 = mybir.dt.bfloat16
+I32 = mybir.dt.int32
+U32 = mybir.dt.uint32
+U16 = mybir.dt.uint16
+U8 = mybir.dt.uint8
+FP8X4 = mybir.dt.float8_e4m3fn_x4
+ACT = mybir.ActivationFunctionType
+ALU = mybir.AluOpType
+
+P = 128
+PACK = 4
+TILES = 4
+CHUNK = 128
+CHUNKS = S // CHUNK
+STRIPE = 16
+HALF = H // 2
+
+
+def tile_picked_twhtriebpage_none_p_kernel(
+    tc, x_words, x_scales, w1, w2, gn, w3, mem, offs, hz, n1, n2, n3, out
+):
+    nc = tc.nc
+    with ExitStack() as ctx:
+        keep = ctx.enter_context(tc.tile_pool(name="keep", bufs=1))
+        ring = ctx.enter_context(tc.tile_pool(name="ring", bufs=2))
+        psum = ctx.enter_context(tc.psum_pool(name="psum", bufs=1))
+        banks = [psum.tile([P, 512], F32, name="bank%d" % b) for b in range(8)]
+
+        def load_list(name, src):
+            tile = keep.tile([P, S // STRIPE], U16, name=name)
+            nc.sync.dma_start(tile[:], src)
+            return tile
+
+        def load_weight(name, w, h):
+            raw = keep.tile([P, PACK, HALF], F32, name=name, tag=name)
+            nc.sync.dma_start(raw[:], w[:, HALF * h : HALF * (h + 1)].rearrange("(p j) c -> p j c", j=PACK))
+            return raw
+
+        xs = keep.tile([P, T], U8, name="xs", align_bytes=64)
+        xs_words = xs[:].bitcast(I32)
+        nc.gpsimd.memset(xs_words, 0)
+        scale_rows = x_scales[0].bitcast(I32)
+        for s in range(2):
+            nc.sync.dma_start(xs_words[s:P:16, :], scale_rows[s:16:2, :])
+        for s in range(2, 4):
+            nc.sync.dma_start(xs_words[s:P:32, :], scale_rows[s:16:4, :])
+        hz_t = load_list("hz_t", hz)
+        offs_t = load_list("offs_t", offs)
+        w1_raw = [load_weight("w1_raw0", w1, 0)]
+        xw = keep.tile([P, T], I32, name="xw", align_bytes=64)
+        nc.sync.dma_start(xw[:], x_words[0].rearrange("p n t -> p (n t)").bitcast(I32))
+        w1_raw.append(load_weight("w1_raw1", w1, 1))
+        gain = keep.tile([P, TILES], F32, name="gain")
+        with nc.allow_non_contiguous_dma(reason="one gain a partition and tile"):
+            nc.scalar.dma_start(gain[:], gn.rearrange("(t p) o -> p (t o)", p=P))
+        w2_raw = [load_weight("slot0", w2, 0)]
+        w2_raw.append(load_weight("slot1", w2, 1))
+        n1_t = load_list("n1_t", n1)
+        n2_t = load_list("n2_t", n2)
+        w3_raw = [load_weight("slot2", w3, 0)]
+        w3_raw.append(load_weight("slot3", w3, 1))
+        n3_t = load_list("n3_t", n3)
+        mem_rows = mem.rearrange("(p t) u -> t p u", t=TILES)
+        out_rows = out.rearrange("(p t) u -> t p u", t=TILES)
+        pages = []
+
+        def load_page(t):
+            page = keep.tile([P, U], F32, name="page%d" % t, tag="slot%d" % t)
+            nc.sync.dma_start(page[:], mem_rows[t])
+            pages.append(page)
+
+        ident = keep.tile([P, P], F32, name="ident")
+        make_identity(nc, ident[:])
+
+        def pool_round(dst, src):
+            nc.gpsimd.tensor_scalar(dst, src, 1.0, 0.0, ALU.mult, ALU.add)
+
+        def round_half(copy, name, raw, tag):
+            grouped = keep.tile([P, PACK * HALF], BF16, name=name, tag=tag, align_bytes=64)
+            copy(
+                grouped[:].rearrange("p (c i j) -> p c j i", i=4, j=PACK),
+                raw[:].rearrange("p j (c i) -> p c j i", i=4),
+            )
+            return grouped
+
+        def quantize(name, grouped):
+            width = grouped.shape[1] // PACK
+            codes = keep.tile([P, width], U32, name=name + "_codes", align_bytes=64)
+            scales = keep.tile([P, width], U8, name=name + "_scales", align_bytes=64)
+            nc.vector.quantize_mx(out=codes[:].bitcast(FP8X4), scales=scales[:], in_=grouped[:])
+            return codes, scales
+
+        def product(target, left, col, right):
+            nc.tensor.matmul_mx(
+                out=target,
+                lhsT=left[0][:, col : col + P].bitcast(FP8X4),
+                lhsT_scale=left[1][:, col : col + P],
+                rhs=right[0][:].bitcast(FP8X4),
+                rhs_scale=right[1][:],
+                start=True,
+                stop=True,
+            )
+
+        hz_bytes = keep.tile([P, S], U8, name="hz_bytes", align_bytes=64)
+        nc.vector.tensor_copy(hz_bytes[:], xs[:].indirect(hz_t[:]))
+        offs_plane = keep.tile([P, S], U8, name="offs_plane", align_bytes=64)
+        nc.vector.tensor_copy(offs_plane[:], xs[:].indirect(offs_t[:]))
+        offs_words = keep.tile([P, S], U32, name="offs_words", align_bytes=64)
+        nc.vector.tensor_copy(offs_words[:], xw[:].bitcast(U32).indirect(offs_t[:]))
+
+        w1_mx = [quantize("w1_0", round_half(nc.scalar.copy, "w1_grouped0", w1_raw[0], "first_half"))]
+        hz_plane = keep.tile([P, S], U8, name="hz_plane", tag="first_half", align_bytes=64)
+        nc.vector.tensor_copy(hz_plane[:].bitcast(I32), hz_bytes[:].bitcast(I32))
+        for s in range(2):
+            nc.scalar.dma_start(hz_plane[:].bitcast(I32)[2 + s : P : 32, :], hz_bytes[:].bitcast(I32)[16 + s : P : 32, :])
+        hz_words = keep.tile([P, S], U32, name="hz_words", align_bytes=64)
+        nc.vector.tensor_copy(hz_words[:], xw[:].bitcast(U32).indirect(hz_t[:]))
+        w1_mx.append(quantize("w1_1", round_half(nc.scalar.copy, "w1_grouped1", w1_raw[1], "")))
+        w2_grouped = [round_half(nc.vector.tensor_copy, "w2_grouped0", w2_raw[0], "")]
+
+        y_rows = []
+        for t in range(TILES):
+            product(banks[t][:], w1_mx[t // 2], P * (t % 2), (offs_words, offs_plane))
+            row = keep.tile([P, S], F32, name="y%d" % t, tag="w1_raw1" if t == 0 else "")
+            nc.scalar.activation(row[:], banks[t][:], ACT.Copy, scale=gain[:, t : t + 1])
+            y_rows.append(row)
+
+        w2_grouped.append(round_half(nc.vector.tensor_copy, "w2_grouped1", w2_raw[1], ""))
+        w2_mx = [quantize("w2_%d" % h, w2_grouped[h]) for h in range(2)]
+        load_page(0)
+        load_page(1)
+
+        h_rows = keep.tile([P, TILES, S], F32, name="h_rows")
+
+        def fetch(name, slot, vector_tiles, rows_of, index, c):
+            near = keep.tile([P, TILES, CHUNK], F32, name="%s%d" % (name, c), tag=slot, align_bytes=64)
+            entries = index[:, CHUNK * c // STRIPE : CHUNK * (c + 1) // STRIPE]
+            for t in range(TILES):
+                if t in vector_tiles:
+                    nc.vector.tensor_copy(near[:, t, :], rows_of[t][:].indirect(entries))
+                else:
+                    nc.scalar.activation(near[:, t, :], rows_of[t][:].indirect(entries), ACT.Copy)
+            return near
+
+        def turned_sum(bank, rows_of, near, c):
+            for t in range(TILES):
+                for first, src in ((True, rows_of[t][:, CHUNK * c : CHUNK * (c + 1)]), (False, near[:, t, :])):
+                    nc.tensor.matmul(bank[:, P * t : P * (t + 1)], src, ident[:], start=first, stop=not first, is_transpose=True)
+
+        def in_pair_order(bank):
+            return bank[:].rearrange("j (p u e) -> j u p e", u=2, e=2)
+
+        def as_pairs(tile):
+            return tile[:].rearrange("j (u p e) -> j u p e", u=2, e=2)
+
+        y_bank = [banks[6] for c in range(CHUNKS)]
+        d_bank = [banks[4 + c % 2] for c in range(CHUNKS)]
+        z_bank = banks[2]
+        y_on_vector = ((), (), (), ())
+        d_on_vector = ((0, 1), (0, 1, 2, 3), (), ())
+
+        def y_fetch(c):
+            return fetch("y_near", "y_slot%d" % (c % 2), y_on_vector[c], y_rows, n1_t, c)
+
+        def d_fetch(c):
+            return fetch("d_near", "sig_slot%d" % (c - 2), d_on_vector[c], d_rows, n2_t, c)
+
+        def gate(c):
+            sig = keep.tile([P, H], F32, name="sig%d" % c, tag="sig_slot%d" % c, align_bytes=64)
+            nc.scalar.activation(as_pairs(sig), in_pair_order(d_bank[c]), ACT.Sigmoid)
+            z_rows = ring.tile([P, H], BF16, name="z_rows")
+            nc.vector.tensor_tensor(as_pairs(z_rows), in_pair_order(y_bank[c]), as_pairs(sig), ALU.mult)
+            return z_rows
+
+        def turn_back(c, z_rows):
+            pairs = z_rows[:].bitcast(F32)
+            for u in range(2):
+                nc.tensor.transpose(z_bank[:, CHUNK * u : CHUNK * (u + 1)], pairs[:, P * u : P * (u + 1)], ident[:])
+            z_grouped = keep.tile([P, PACK * CHUNK], BF16, name="z_grouped%d" % c, tag="z_slot%d" % c, align_bytes=64)
+            nc.scalar.copy(
+                z_grouped[:].bitcast(F32).rearrange("p (j u) -> p j u", u=2),
+                z_bank[:, : 2 * CHUNK].rearrange("p (u j) -> p j u", u=2),
+            )
+            return quantize("z%d" % c, z_grouped)
+
+        def last_product(c, z_mx, bank, t0, t1):
+            for t in range(t0, t1):
+                product(bank[:, CHUNK * (t - t0) : CHUNK * (t - t0 + 1)], w3_mx, P * t, z_mx)
+            nc.scalar.copy(
+                h_rows[:, t0:t1, CHUNK * c : CHUNK * (c + 1)],
+                bank[:, : (t1 - t0) * CHUNK].rearrange("p (t j) -> p t j", j=CHUNK),
+            )
+
+        def put(t, c0, c1):
+            entries = n3_t[:, CHUNK * c0 // STRIPE : CHUNK * c1 // STRIPE]
+            nc.vector.tensor_copy(pages[t][:].indirect(entries), h_rows[:, t, CHUNK * c0 : CHUNK * c1])
+            if c1 == CHUNKS:
+                nc.sync.dma_start(out_rows[t], pages[t][:])
+
+        y_near = y_fetch(0)
+        d_rows = []
+        for t in range(TILES):
+            product(banks[4 + t][:], w2_mx[t // 2], P * (t % 2), (hz_words, hz_plane))
+            row = keep.tile([P, S], F32, name="d%d" % t)
+            if t in (0, 1, 2):
+                nc.vector.tensor_copy(row[:], banks[4 + t][:])
+            else:
+                nc.scalar.copy(row[:], banks[4 + t][:])
+            d_rows.append(row)
+        turned_sum(d_bank[0], d_rows, d_fetch(0), 0)
+        turned_sum(y_bank[0], y_rows, y_near, 0)
+        z_rows = gate(0)
+
+        w3_grouped = keep.tile([P, PACK * N], BF16, name="w3_grouped", align_bytes=64)
+        dealt = w3_grouped[:].rearrange("p (t m j) -> p m j t", t=TILES, j=PACK)
+        for h in range(2):
+            nc.vector.tensor_copy(dealt[:, P // 2 * h : P // 2 * (h + 1)], w3_raw[h][:].rearrange("p j (m t) -> p m j t", t=TILES))
+            load_page(2 + h)
+        w3_mx = quantize("w3", w3_grouped)
+
+        def sums(c):
+            turned_sum(d_bank[c], d_rows, d_fetch(c), c)
+            turned_sum(y_bank[c], y_rows, y_fetch(c), c)
+
+        z_mx = turn_back(0, z_rows)
+        sums(1)
+        for c in range(CHUNKS):
+            last = c + 1 == CHUNKS
+            free = 1 if c == 0 else 0
+            if free:
+                last_product(c, z_mx, banks[3], 0, free)
+            if not last:
+                z_rows = gate(c + 1)
+            if free < 2:
+                last_product(c, z_mx, d_bank[min(c + 1, CHUNKS - 1)], free, 2)
+            put(0, c, c + 1)
+            put(1, c, c + 1)
+            if not last:
+                z_next = turn_back(c + 1, z_rows)
+            last_product(c, z_mx, z_bank, 2, 4)
+            if c + 2 < CHUNKS:
+                sums(c + 2)
+            put(2, c, c + 1)
+            if c < CHUNKS - 2:
+                put(3, c, c + 1)
+            elif last:
+                put(3, c - 1, c + 1)
+            z_mx = z_next

@@ -19,7 +19,8 @@ ALU = mybir.AluOpType
 P = 128
 PACK = 4
 TILES = 4
-CHUNK = 128
+CHUNK = 256
+BLOCKS = CHUNK // P
 CHUNKS = S // CHUNK
 STRIPE = 16
 HALF = H // 2
@@ -48,6 +49,9 @@ def tile_picked_twhtriebpage_none_p_kernel(
         xs = keep.tile([P, T], U8, name="xs", align_bytes=64)
         xs_words = xs[:].bitcast(I32)
         nc.gpsimd.memset(xs_words, 0)
+        warm = keep.tile([P, 2], F32, name="warm")
+        nc.vector.memset(warm[:, 0:1], 0.0)
+        nc.scalar.activation(warm[:, 1:2], warm[:, 0:1], ACT.Sigmoid)
         scale_rows = x_scales[0].bitcast(I32)
         for s in range(2):
             nc.sync.dma_start(xs_words[s:P:16, :], scale_rows[s:16:2, :])
@@ -59,10 +63,10 @@ def tile_picked_twhtriebpage_none_p_kernel(
         xw = keep.tile([P, T], I32, name="xw", align_bytes=64)
         nc.sync.dma_start(xw[:], x_words[0].rearrange("p n t -> p (n t)").bitcast(I32))
         w1_raw.append(load_weight("w1_raw1", w1, 1))
+        w2_raw = [load_weight("slot0", w2, 0)]
         gain = keep.tile([P, TILES], F32, name="gain")
         with nc.allow_non_contiguous_dma(reason="one gain a partition and tile"):
-            nc.scalar.dma_start(gain[:], gn.rearrange("(t p) o -> p (t o)", p=P))
-        w2_raw = [load_weight("slot0", w2, 0)]
+            nc.sync.dma_start(gain[:], gn.rearrange("(t p) o -> p (t o)", p=P))
         w2_raw.append(load_weight("slot1", w2, 1))
         n1_t = load_list("n1_t", n1)
         n2_t = load_list("n2_t", n2)
@@ -124,8 +128,8 @@ def tile_picked_twhtriebpage_none_p_kernel(
             nc.scalar.dma_start(hz_plane[:].bitcast(I32)[2 + s : P : 32, :], hz_bytes[:].bitcast(I32)[16 + s : P : 32, :])
         hz_words = keep.tile([P, S], U32, name="hz_words", align_bytes=64)
         nc.vector.tensor_copy(hz_words[:], xw[:].bitcast(U32).indirect(hz_t[:]))
-        w1_mx.append(quantize("w1_1", round_half(nc.scalar.copy, "w1_grouped1", w1_raw[1], "")))
-        w2_grouped = [round_half(nc.vector.tensor_copy, "w2_grouped0", w2_raw[0], "")]
+        w1_mx.append(quantize("w1_1", round_half(nc.scalar.copy, "w1_grouped1", w1_raw[1], "second_half")))
+        w2_grouped = [round_half(nc.vector.tensor_copy, "w2_grouped0", w2_raw[0], "second_half")]
 
         y_rows = []
         for t in range(TILES):
@@ -134,27 +138,34 @@ def tile_picked_twhtriebpage_none_p_kernel(
             nc.scalar.activation(row[:], banks[t][:], ACT.Copy, scale=gain[:, t : t + 1])
             y_rows.append(row)
 
-        w2_grouped.append(round_half(nc.vector.tensor_copy, "w2_grouped1", w2_raw[1], ""))
+        w2_grouped.append(round_half(nc.vector.tensor_copy, "w2_grouped1", w2_raw[1], "last_half"))
         w2_mx = [quantize("w2_%d" % h, w2_grouped[h]) for h in range(2)]
         load_page(0)
         load_page(1)
 
         h_rows = keep.tile([P, TILES, S], F32, name="h_rows")
 
-        def fetch(name, slot, vector_tiles, rows_of, index, c):
-            near = keep.tile([P, TILES, CHUNK], F32, name="%s%d" % (name, c), tag=slot, align_bytes=64)
-            entries = index[:, CHUNK * c // STRIPE : CHUNK * (c + 1) // STRIPE]
-            for t in range(TILES):
-                if t in vector_tiles:
-                    nc.vector.tensor_copy(near[:, t, :], rows_of[t][:].indirect(entries))
-                else:
-                    nc.scalar.activation(near[:, t, :], rows_of[t][:].indirect(entries), ACT.Copy)
-            return near
+        fetched = {}
 
-        def turned_sum(bank, rows_of, near, c):
-            for t in range(TILES):
-                for first, src in ((True, rows_of[t][:, CHUNK * c : CHUNK * (c + 1)]), (False, near[:, t, :])):
-                    nc.tensor.matmul(bank[:, P * t : P * (t + 1)], src, ident[:], start=first, stop=not first, is_transpose=True)
+        def fetch(name, plan, rows_of, index, c):
+            entries = index[:, CHUNK * c // STRIPE : CHUNK * (c + 1) // STRIPE]
+            for tiles, on_vector, slot in plan:
+                near = keep.tile([P, len(tiles), CHUNK], F32, name="%s%d_%d" % (name, c, tiles[0]), tag=slot, align_bytes=64)
+                for k, t in enumerate(tiles):
+                    if on_vector:
+                        nc.vector.tensor_copy(near[:, k, :], rows_of[t][:].indirect(entries))
+                    else:
+                        nc.scalar.activation(near[:, k, :], rows_of[t][:].indirect(entries), ACT.Copy)
+                    fetched[name, c, t] = near[:, k, :]
+
+        def turned_sum(bank, rows_of, name, c, b):
+            order = range(TILES) if name == "d_near" else range(TILES)
+            terms = [(t, rows_of[t][:, CHUNK * c + P * b : CHUNK * c + P * (b + 1)]) for t in range(TILES)]
+            terms = terms + [(t, fetched[name, c, t][:, P * b : P * (b + 1)]) for t in order]
+            for k, (t, src) in enumerate(terms):
+                nc.tensor.matmul(
+                    bank[:, P * t : P * (t + 1)], src, ident[:], start=k == 0, stop=k == len(terms) - 1, is_transpose=True
+                )
 
         def in_pair_order(bank):
             return bank[:].rearrange("j (p u e) -> j u p e", u=2, e=2)
@@ -162,62 +173,68 @@ def tile_picked_twhtriebpage_none_p_kernel(
         def as_pairs(tile):
             return tile[:].rearrange("j (u p e) -> j u p e", u=2, e=2)
 
-        y_bank = [banks[6] for c in range(CHUNKS)]
-        d_bank = [banks[4 + c % 2] for c in range(CHUNKS)]
-        z_bank = banks[2]
-        y_on_vector = ((), (), (), ())
-        d_on_vector = ((0, 1), (0, 1, 2, 3), (), ())
+        d_bank, y_bank, z_bank = banks[4:6], banks[0:2], banks[2]
 
-        def y_fetch(c):
-            return fetch("y_near", "y_slot%d" % (c % 2), y_on_vector[c], y_rows, n1_t, c)
-
-        def d_fetch(c):
-            return fetch("d_near", "sig_slot%d" % (c - 2), d_on_vector[c], d_rows, n2_t, c)
+        def sums(c):
+            for b in range(BLOCKS):
+                turned_sum(d_bank[b], d_rows, "d_near", c, b)
+            for b in range(BLOCKS):
+                turned_sum(y_bank[b], y_rows, "y_near", c, b)
 
         def gate(c):
-            sig = keep.tile([P, H], F32, name="sig%d" % c, tag="sig_slot%d" % c, align_bytes=64)
-            nc.scalar.activation(as_pairs(sig), in_pair_order(d_bank[c]), ACT.Sigmoid)
-            z_rows = ring.tile([P, H], BF16, name="z_rows")
-            nc.vector.tensor_tensor(as_pairs(z_rows), in_pair_order(y_bank[c]), as_pairs(sig), ALU.mult)
+            z_rows = []
+            for b in range(BLOCKS):
+                sig = keep.tile([P, H], F32, name="sig%d_%d" % (c, b), tag="sig_slot%d_%d" % (c, b), align_bytes=64)
+                nc.scalar.activation(as_pairs(sig), in_pair_order(d_bank[b]), ACT.Sigmoid)
+                rows = keep.tile([P, H], BF16, name="z_rows%d_%d" % (c, b), tag="row_slot%d_%d" % (c, b), align_bytes=64)
+                nc.vector.tensor_tensor(as_pairs(rows), in_pair_order(y_bank[b]), as_pairs(sig), ALU.mult)
+                z_rows.append(rows)
             return z_rows
 
-        def turn_back(c, z_rows):
-            pairs = z_rows[:].bitcast(F32)
-            for u in range(2):
-                nc.tensor.transpose(z_bank[:, CHUNK * u : CHUNK * (u + 1)], pairs[:, P * u : P * (u + 1)], ident[:])
-            z_grouped = keep.tile([P, PACK * CHUNK], BF16, name="z_grouped%d" % c, tag="z_slot%d" % c, align_bytes=64)
+        def turn_back(name, z_rows, bank):
+            width = P * len(z_rows)
+            for b, rows in enumerate(z_rows):
+                pairs = rows[:].bitcast(F32)
+                for u in range(2):
+                    col = width * u + P * b
+                    nc.tensor.transpose(bank[:, col : col + P], pairs[:, P * u : P * (u + 1)], ident[:])
+            z_grouped = keep.tile([P, PACK * width], BF16, name="z_grouped" + name, tag="z_slot" + name, align_bytes=64)
             nc.scalar.copy(
                 z_grouped[:].bitcast(F32).rearrange("p (j u) -> p j u", u=2),
-                z_bank[:, : 2 * CHUNK].rearrange("p (u j) -> p j u", u=2),
+                bank[:, : 2 * width].rearrange("p (u j) -> p j u", u=2),
             )
-            return quantize("z%d" % c, z_grouped)
+            return quantize("z" + name, z_grouped)
 
-        def last_product(c, z_mx, bank, t0, t1):
-            for t in range(t0, t1):
-                product(bank[:, CHUNK * (t - t0) : CHUNK * (t - t0 + 1)], w3_mx, P * t, z_mx)
+        def last_product(parts, bank, tiles, j0):
+            width = sum(part[0].shape[1] for part in parts)
+            for k, t in enumerate(tiles):
+                col = width * k
+                for part in parts:
+                    product(bank[:, col : col + part[0].shape[1]], w3_mx, P * t, part)
+                    col = col + part[0].shape[1]
             nc.scalar.copy(
-                h_rows[:, t0:t1, CHUNK * c : CHUNK * (c + 1)],
-                bank[:, : (t1 - t0) * CHUNK].rearrange("p (t j) -> p t j", j=CHUNK),
+                h_rows[:, tiles[0] : tiles[-1] + 1, j0 : j0 + width],
+                bank[:, : len(tiles) * width].rearrange("p (t j) -> p t j", j=width),
             )
 
-        def put(t, c0, c1):
-            entries = n3_t[:, CHUNK * c0 // STRIPE : CHUNK * c1 // STRIPE]
-            nc.vector.tensor_copy(pages[t][:].indirect(entries), h_rows[:, t, CHUNK * c0 : CHUNK * c1])
-            if c1 == CHUNKS:
+        def put(t, j0, j1):
+            nc.vector.tensor_copy(pages[t][:].indirect(n3_t[:, j0 // STRIPE : j1 // STRIPE]), h_rows[:, t, j0:j1])
+            if j1 == S:
                 nc.sync.dma_start(out_rows[t], pages[t][:])
 
-        y_near = y_fetch(0)
+        fetch("y_near", [((0,), True, "last_half")], y_rows, n1_t, 0)
         d_rows = []
         for t in range(TILES):
             product(banks[4 + t][:], w2_mx[t // 2], P * (t % 2), (hz_words, hz_plane))
             row = keep.tile([P, S], F32, name="d%d" % t)
-            if t in (0, 1, 2):
+            if t in (2, 3):
                 nc.vector.tensor_copy(row[:], banks[4 + t][:])
             else:
                 nc.scalar.copy(row[:], banks[4 + t][:])
             d_rows.append(row)
-        turned_sum(d_bank[0], d_rows, d_fetch(0), 0)
-        turned_sum(y_bank[0], y_rows, y_near, 0)
+        fetch("d_near", [((0, 1), False, "d_pair"), ((2, 3), True, "first_d")], d_rows, n2_t, 0)
+        fetch("y_near", [((1, 2, 3), False, "")], y_rows, n1_t, 0)
+        sums(0)
         z_rows = gate(0)
 
         w3_grouped = keep.tile([P, PACK * N], BF16, name="w3_grouped", align_bytes=64)
@@ -227,31 +244,22 @@ def tile_picked_twhtriebpage_none_p_kernel(
             load_page(2 + h)
         w3_mx = quantize("w3", w3_grouped)
 
-        def sums(c):
-            turned_sum(d_bank[c], d_rows, d_fetch(c), c)
-            turned_sum(y_bank[c], y_rows, y_fetch(c), c)
-
-        z_mx = turn_back(0, z_rows)
+        z_first = []
+        for b in range(BLOCKS):
+            z_first.append(turn_back("0%d" % b, z_rows[b : b + 1], banks[2 + b]))
+            last_product(z_first[b : b + 1], banks[6 + b], (0, 1), P * b)
+        fetch("d_near", [((0, 1), False, "row_slot0_0"), ((2, 3), True, "z_slot00")], d_rows, n2_t, 1)
+        fetch("y_near", [((3,), True, "sig_slot0_1"), ((0, 1, 2), False, "z_slot01")], y_rows, n1_t, 1)
+        for b in range(BLOCKS):
+            for t in range(2):
+                put(t, P * b, P * (b + 1))
         sums(1)
-        for c in range(CHUNKS):
-            last = c + 1 == CHUNKS
-            free = 1 if c == 0 else 0
-            if free:
-                last_product(c, z_mx, banks[3], 0, free)
-            if not last:
-                z_rows = gate(c + 1)
-            if free < 2:
-                last_product(c, z_mx, d_bank[min(c + 1, CHUNKS - 1)], free, 2)
-            put(0, c, c + 1)
-            put(1, c, c + 1)
-            if not last:
-                z_next = turn_back(c + 1, z_rows)
-            last_product(c, z_mx, z_bank, 2, 4)
-            if c + 2 < CHUNKS:
-                sums(c + 2)
-            put(2, c, c + 1)
-            if c < CHUNKS - 2:
-                put(3, c, c + 1)
-            elif last:
-                put(3, c - 1, c + 1)
-            z_mx = z_next
+        z_rows = gate(1)
+        last_product(z_first, d_bank[1], (2,), 0)
+        put(2, 0, CHUNK)
+        z_last = turn_back("1", z_rows, z_bank)
+        last_product(z_first, z_bank, (3,), 0)
+        put(3, 0, CHUNK)
+        for t in range(TILES):
+            last_product([z_last], banks[6 + t % 2], (t,), CHUNK)
+            put(t, CHUNK, S)

from contextlib import ExitStack

import concourse.mybir as mybir
from concourse.masks import make_identity

K, T, S, N, H, U = 512, 2048, 512, 512, 512, 1024
FLOPS = 2 * S * (K * H + K * H + H * N)

F32 = mybir.dt.float32
BF16 = mybir.dt.bfloat16
I32 = mybir.dt.int32
U32 = mybir.dt.uint32
U16 = mybir.dt.uint16
U8 = mybir.dt.uint8
FP8X4 = mybir.dt.float8_e4m3fn_x4
ACT = mybir.ActivationFunctionType
ALU = mybir.AluOpType

P = 128
PACK = 4
TILES = 4
CHUNK = 256
BLOCKS = CHUNK // P
CHUNKS = S // CHUNK
STRIPE = 16
HALF = H // 2


def tile_picked_twhtriebpage_none_p_kernel(
    tc, x_words, x_scales, w1, w2, gn, w3, mem, offs, hz, n1, n2, n3, out
):
    nc = tc.nc
    with ExitStack() as ctx:
        keep = ctx.enter_context(tc.tile_pool(name="keep", bufs=1))
        ring = ctx.enter_context(tc.tile_pool(name="ring", bufs=2))
        psum = ctx.enter_context(tc.psum_pool(name="psum", bufs=1))
        banks = [psum.tile([P, 512], F32, name="bank%d" % b) for b in range(8)]

        def load_list(name, src):
            tile = keep.tile([P, S // STRIPE], U16, name=name)
            nc.sync.dma_start(tile[:], src)
            return tile

        def load_weight(name, w, h):
            raw = keep.tile([P, PACK, HALF], F32, name=name, tag=name)
            nc.sync.dma_start(raw[:], w[:, HALF * h : HALF * (h + 1)].rearrange("(p j) c -> p j c", j=PACK))
            return raw

        xs = keep.tile([P, T], U8, name="xs", align_bytes=64)
        xs_words = xs[:].bitcast(I32)
        nc.gpsimd.memset(xs_words, 0)
        warm = keep.tile([P, 2], F32, name="warm")
        nc.vector.memset(warm[:, 0:1], 0.0)
        nc.scalar.activation(warm[:, 1:2], warm[:, 0:1], ACT.Sigmoid)
        scale_rows = x_scales[0].bitcast(I32)
        for s in range(2):
            nc.sync.dma_start(xs_words[s:P:16, :], scale_rows[s:16:2, :])
        for s in range(2, 4):
            nc.sync.dma_start(xs_words[s:P:32, :], scale_rows[s:16:4, :])
        hz_t = load_list("hz_t", hz)
        offs_t = load_list("offs_t", offs)
        w1_raw = [load_weight("w1_raw0", w1, 0)]
        xw = keep.tile([P, T], I32, name="xw", align_bytes=64)
        nc.sync.dma_start(xw[:], x_words[0].rearrange("p n t -> p (n t)").bitcast(I32))
        w1_raw.append(load_weight("w1_raw1", w1, 1))
        w2_raw = [load_weight("slot0", w2, 0)]
        gain = keep.tile([P, TILES], F32, name="gain")
        with nc.allow_non_contiguous_dma(reason="one gain a partition and tile"):
            nc.sync.dma_start(gain[:], gn.rearrange("(t p) o -> p (t o)", p=P))
        w2_raw.append(load_weight("slot1", w2, 1))
        n1_t = load_list("n1_t", n1)
        n2_t = load_list("n2_t", n2)
        w3_raw = [load_weight("slot2", w3, 0)]
        w3_raw.append(load_weight("slot3", w3, 1))
        n3_t = load_list("n3_t", n3)
        mem_rows = mem.rearrange("(p t) u -> t p u", t=TILES)
        out_rows = out.rearrange("(p t) u -> t p u", t=TILES)
        pages = []

        def load_page(t):
            page = keep.tile([P, U], F32, name="page%d" % t, tag="slot%d" % t)
            nc.sync.dma_start(page[:], mem_rows[t])
            pages.append(page)

        ident = keep.tile([P, P], F32, name="ident")
        make_identity(nc, ident[:])

        def pool_round(dst, src):
            nc.gpsimd.tensor_scalar(dst, src, 1.0, 0.0, ALU.mult, ALU.add)

        def round_half(copy, name, raw, tag):
            grouped = keep.tile([P, PACK * HALF], BF16, name=name, tag=tag, align_bytes=64)
            copy(
                grouped[:].rearrange("p (c i j) -> p c j i", i=4, j=PACK),
                raw[:].rearrange("p j (c i) -> p c j i", i=4),
            )
            return grouped

        def quantize(name, grouped):
            width = grouped.shape[1] // PACK
            codes = keep.tile([P, width], U32, name=name + "_codes", align_bytes=64)
            scales = keep.tile([P, width], U8, name=name + "_scales", align_bytes=64)
            nc.vector.quantize_mx(out=codes[:].bitcast(FP8X4), scales=scales[:], in_=grouped[:])
            return codes, scales

        def product(target, left, col, right):
            nc.tensor.matmul_mx(
                out=target,
                lhsT=left[0][:, col : col + P].bitcast(FP8X4),
                lhsT_scale=left[1][:, col : col + P],
                rhs=right[0][:].bitcast(FP8X4),
                rhs_scale=right[1][:],
                start=True,
                stop=True,
            )

        hz_bytes = keep.tile([P, S], U8, name="hz_bytes", align_bytes=64)
        nc.vector.tensor_copy(hz_bytes[:], xs[:].indirect(hz_t[:]))
        offs_plane = keep.tile([P, S], U8, name="offs_plane", align_bytes=64)
        nc.vector.tensor_copy(offs_plane[:], xs[:].indirect(offs_t[:]))
        offs_words = keep.tile([P, S], U32, name="offs_words", align_bytes=64)
        nc.vector.tensor_copy(offs_words[:], xw[:].bitcast(U32).indirect(offs_t[:]))

        w1_mx = [quantize("w1_0", round_half(nc.scalar.copy, "w1_grouped0", w1_raw[0], "first_half"))]
        hz_plane = keep.tile([P, S], U8, name="hz_plane", tag="first_half", align_bytes=64)
        nc.vector.tensor_copy(hz_plane[:].bitcast(I32), hz_bytes[:].bitcast(I32))
        for s in range(2):
            nc.scalar.dma_start(hz_plane[:].bitcast(I32)[2 + s : P : 32, :], hz_bytes[:].bitcast(I32)[16 + s : P : 32, :])
        hz_words = keep.tile([P, S], U32, name="hz_words", align_bytes=64)
        nc.vector.tensor_copy(hz_words[:], xw[:].bitcast(U32).indirect(hz_t[:]))
        w1_mx.append(quantize("w1_1", round_half(nc.scalar.copy, "w1_grouped1", w1_raw[1], "second_half")))
        w2_grouped = [round_half(nc.vector.tensor_copy, "w2_grouped0", w2_raw[0], "second_half")]

        y_rows = []
        for t in range(TILES):
            product(banks[t][:], w1_mx[t // 2], P * (t % 2), (offs_words, offs_plane))
            row = keep.tile([P, S], F32, name="y%d" % t, tag="w1_raw1" if t == 0 else "")
            nc.scalar.activation(row[:], banks[t][:], ACT.Copy, scale=gain[:, t : t + 1])
            y_rows.append(row)

        w2_grouped.append(round_half(nc.vector.tensor_copy, "w2_grouped1", w2_raw[1], "last_half"))
        w2_mx = [quantize("w2_%d" % h, w2_grouped[h]) for h in range(2)]
        load_page(0)
        load_page(1)

        h_rows = keep.tile([P, TILES, S], F32, name="h_rows")

        fetched = {}

        def fetch(name, plan, rows_of, index, c):
            entries = index[:, CHUNK * c // STRIPE : CHUNK * (c + 1) // STRIPE]
            for tiles, on_vector, slot in plan:
                near = keep.tile([P, len(tiles), CHUNK], F32, name="%s%d_%d" % (name, c, tiles[0]), tag=slot, align_bytes=64)
                for k, t in enumerate(tiles):
                    if on_vector:
                        nc.vector.tensor_copy(near[:, k, :], rows_of[t][:].indirect(entries))
                    else:
                        nc.scalar.activation(near[:, k, :], rows_of[t][:].indirect(entries), ACT.Copy)
                    fetched[name, c, t] = near[:, k, :]

        def turned_sum(bank, rows_of, name, c, b):
            order = range(TILES) if name == "d_near" else range(TILES)
            terms = [(t, rows_of[t][:, CHUNK * c + P * b : CHUNK * c + P * (b + 1)]) for t in range(TILES)]
            terms = terms + [(t, fetched[name, c, t][:, P * b : P * (b + 1)]) for t in order]
            for k, (t, src) in enumerate(terms):
                nc.tensor.matmul(
                    bank[:, P * t : P * (t + 1)], src, ident[:], start=k == 0, stop=k == len(terms) - 1, is_transpose=True
                )

        def in_pair_order(bank):
            return bank[:].rearrange("j (p u e) -> j u p e", u=2, e=2)

        def as_pairs(tile):
            return tile[:].rearrange("j (u p e) -> j u p e", u=2, e=2)

        d_bank, y_bank, z_bank = banks[4:6], banks[0:2], banks[2]

        def sums(c):
            for b in range(BLOCKS):
                turned_sum(d_bank[b], d_rows, "d_near", c, b)
            for b in range(BLOCKS):
                turned_sum(y_bank[b], y_rows, "y_near", c, b)

        def gate(c):
            z_rows = []
            for b in range(BLOCKS):
                sig = keep.tile([P, H], F32, name="sig%d_%d" % (c, b), tag="sig_slot%d_%d" % (c, b), align_bytes=64)
                nc.scalar.activation(as_pairs(sig), in_pair_order(d_bank[b]), ACT.Sigmoid)
                rows = keep.tile([P, H], BF16, name="z_rows%d_%d" % (c, b), tag="row_slot%d_%d" % (c, b), align_bytes=64)
                nc.vector.tensor_tensor(as_pairs(rows), in_pair_order(y_bank[b]), as_pairs(sig), ALU.mult)
                z_rows.append(rows)
            return z_rows

        def turn_back(name, z_rows, bank):
            width = P * len(z_rows)
            for b, rows in enumerate(z_rows):
                pairs = rows[:].bitcast(F32)
                for u in range(2):
                    col = width * u + P * b
                    nc.tensor.transpose(bank[:, col : col + P], pairs[:, P * u : P * (u + 1)], ident[:])
            z_grouped = keep.tile([P, PACK * width], BF16, name="z_grouped" + name, tag="z_slot" + name, align_bytes=64)
            nc.scalar.copy(
                z_grouped[:].bitcast(F32).rearrange("p (j u) -> p j u", u=2),
                bank[:, : 2 * width].rearrange("p (u j) -> p j u", u=2),
            )
            return quantize("z" + name, z_grouped)

        def last_product(parts, bank, tiles, j0):
            width = sum(part[0].shape[1] for part in parts)
            for k, t in enumerate(tiles):
                col = width * k
                for part in parts:
                    product(bank[:, col : col + part[0].shape[1]], w3_mx, P * t, part)
                    col = col + part[0].shape[1]
            nc.scalar.copy(
                h_rows[:, tiles[0] : tiles[-1] + 1, j0 : j0 + width],
                bank[:, : len(tiles) * width].rearrange("p (t j) -> p t j", j=width),
            )

        def put(t, j0, j1):
            nc.vector.tensor_copy(pages[t][:].indirect(n3_t[:, j0 // STRIPE : j1 // STRIPE]), h_rows[:, t, j0:j1])
            if j1 == S:
                nc.sync.dma_start(out_rows[t], pages[t][:])

        fetch("y_near", [((0,), True, "last_half")], y_rows, n1_t, 0)
        d_rows = []
        for t in range(TILES):
            product(banks[4 + t][:], w2_mx[t // 2], P * (t % 2), (hz_words, hz_plane))
            row = keep.tile([P, S], F32, name="d%d" % t)
            if t in (2, 3):
                nc.vector.tensor_copy(row[:], banks[4 + t][:])
            else:
                nc.scalar.copy(row[:], banks[4 + t][:])
            d_rows.append(row)
        fetch("d_near", [((0, 1), False, "d_pair"), ((2, 3), True, "first_d")], d_rows, n2_t, 0)
        fetch("y_near", [((1, 2, 3), False, "")], y_rows, n1_t, 0)
        sums(0)
        z_rows = gate(0)

        w3_grouped = keep.tile([P, PACK * N], BF16, name="w3_grouped", align_bytes=64)
        dealt = w3_grouped[:].rearrange("p (t m j) -> p m j t", t=TILES, j=PACK)
        for h in range(2):
            nc.vector.tensor_copy(dealt[:, P // 2 * h : P // 2 * (h + 1)], w3_raw[h][:].rearrange("p j (m t) -> p m j t", t=TILES))
            load_page(2 + h)
        w3_mx = quantize("w3", w3_grouped)

        z_first = []
        for b in range(BLOCKS):
            z_first.append(turn_back("0%d" % b, z_rows[b : b + 1], banks[2 + b]))
            last_product(z_first[b : b + 1], banks[6 + b], (0, 1), P * b)
        fetch("d_near", [((0, 1), False, "row_slot0_0"), ((2, 3), True, "z_slot00")], d_rows, n2_t, 1)
        fetch("y_near", [((3,), True, "sig_slot0_1"), ((0, 1, 2), False, "z_slot01")], y_rows, n1_t, 1)
        for b in range(BLOCKS):
            for t in range(2):
                put(t, P * b, P * (b + 1))
        sums(1)
        z_rows = gate(1)
        last_product(z_first, d_bank[1], (2,), 0)
        put(2, 0, CHUNK)
        z_last = turn_back("1", z_rows, z_bank)
        last_product(z_first, z_bank, (3,), 0)
        put(3, 0, CHUNK)
        for t in range(TILES):
            last_product([z_last], banks[6 + t % 2], (t,), CHUNK)
            put(t, CHUNK, S)
